import numpy as np
import ml_dtypes


def mxq(x, axis, fmt="e4m3"):
    dtype, down = {"e4m3": (ml_dtypes.float8_e4m3fn, 7), "e5m2": (ml_dtypes.float8_e5m2, 14)}[fmt]
    v = np.moveaxis(np.asarray(x, np.float32).astype(ml_dtypes.bfloat16).astype(np.float64), axis, -1)
    blocks = v.reshape(v.shape[:-1] + (-1, 32))
    amax = np.abs(blocks).max(-1, keepdims=True)
    byte = np.maximum(np.where(amax > 0, np.frexp(amax)[1] - 1 + 127, 0) - down, 1)
    scale = np.exp2(byte - 127.0)
    codes = (blocks / scale).astype(np.float32).astype(dtype).astype(np.float64)
    return np.moveaxis((codes * scale).reshape(v.shape), -1, axis)


WIDE = False


def mx_kscale(k):
    if not WIDE:
        return np.ones(k)
    levels = np.array([10, -10, 5, -5, 0])
    if k % 512:
        return np.exp2(np.random.permutation(np.resize(levels, k // 32))).repeat(32)
    a = np.empty((k // 512, 16))
    for p in range(k // 512):
        a[p, :8] = np.random.permutation(np.resize(levels, 8))
        for g in range(8):
            far = levels[np.abs(levels - a[p, g]) >= 10]
            a[p, g + 8] = far[np.random.randint(len(far))]
    return np.exp2(a.ravel()).repeat(32)


def f64(x):
    return np.asarray(x).astype(np.float64)


def striped(idx):
    return np.tile(idx.reshape(-1, 16).T, (8, 1)).astype(np.uint16)


def unstriped(offs):
    return offs[:16].T.reshape(-1).astype(np.int64)


def pack_weight(w):
    k, n = w.shape
    w = f64(np.asarray(w, np.float32).astype(ml_dtypes.bfloat16)).reshape(k // 32, 32, n)
    amax = np.abs(w).max(1)
    byte = np.clip(np.where(amax > 0, np.frexp(amax)[1] - 1 + 127 - 7, 1), 1, 254)
    scaled = (w * np.exp2(127.0 - byte)[:, None, :]).reshape(k, n).astype(np.float32)
    words = np.ascontiguousarray(scaled.reshape(k // 512, 128, 4, n).transpose(0, 1, 3, 2)).astype(ml_dtypes.float8_e4m3fn).view(np.uint8)
    return words, np.ascontiguousarray(byte.astype(np.uint8).reshape(k // 512, 16, n))


def unpack_weight(words, scales):
    g, p, n, _ = words.shape
    vals = np.ascontiguousarray(words).view(ml_dtypes.float8_e4m3fn).astype(np.float64) * np.repeat(np.exp2(scales.astype(np.float64) - 127.0), 8, axis=1)[..., None]
    return vals.transpose(0, 1, 3, 2).reshape(g * 512, n)


def planes(y):
    n, m = y.shape
    v = y.astype(np.float32).astype(ml_dtypes.bfloat16).astype(np.float64).reshape(n // 32, 32, m)
    top = np.abs(v).max(1)
    byte = np.clip(np.where(top > 0, np.frexp(top)[1] - 1 + 127 - 7, 1), 1, 254)
    codes = (v * np.exp2(127.0 - byte)[:, None, :]).reshape(n, m).astype(np.float32).astype(ml_dtypes.float8_e4m3fn).view(np.uint8)
    words = codes.reshape(n // 512, 128, 4, m).transpose(0, 1, 3, 2)
    return np.ascontiguousarray(words), np.ascontiguousarray(byte.astype(np.uint8).reshape(n // 512, 16, m))


K, T, S, N, U = 1024, 1024, 512, 512, 1024
P = 2 ** 7


def setup_inputs():
    n = np.random.standard_normal
    s = mx_kscale(K)[:, None]
    packed_xT = pack_weight(n((K, T)) * s)
    return {
        "x_words": packed_xT[0],
        "x_scales": packed_xT[1],
        "cache": (n((N, U))).astype(np.float32),
        "w1": (n((K, N)) / np.sqrt(K) / s).astype(np.float32),
        "scale": (np.tile(np.random.uniform(0.5, 1.5, S), (P, 1))).astype(np.float32),
        "offs": striped(np.random.permutation(T)[:S]),
        "slot": striped(np.random.permutation(U)[:S]),
    }


def reference(x_words, x_scales, cache, w1, scale, offs, slot):
    xq = unpack_weight(x_words, x_scales)[:, unstriped(offs)]
    y = mxq(f64(w1), 0, "e4m3").T @ xq
    r = y * f64(scale)[:1]
    out = f64(cache).copy()
    out[:, unstriped(slot)] = r
    out_0 = out
    return (out_0,) + planes(out_0)

@@ -1,0 +1,199 @@
+from contextlib import ExitStack
+
+import concourse.mybir as mybir
+
+K, T, S, N, U = 1024, 1024, 512, 512, 1024
+FLOPS = 2 * K * N * S
+
+F32 = mybir.dt.float32
+BF16 = mybir.dt.bfloat16
+I32 = mybir.dt.int32
+U32 = mybir.dt.uint32
+U16 = mybir.dt.uint16
+U8 = mybir.dt.uint8
+FP8X4 = mybir.dt.float8_e4m3fn_x4
+COPY = mybir.ActivationFunctionType.Copy
+MULT = mybir.AluOpType.mult
+
+P = 128
+PACK = 4
+K_PASS = P * PACK
+PASSES = K // K_PASS
+HALF = S // 2
+LANES = 16
+M_VECTOR = 80
+LAST_VECTOR = 128
+
+
+def tile_picked_zkvw_none_po_kernel(tc, x_words, x_scales, cache, w1, scale, offs, slot, out_0, out_1, out_2):
+    nc = tc.nc
+    with ExitStack() as ctx:
+        keep = ctx.enter_context(tc.tile_pool(name="keep", bufs=1))
+        psum = ctx.enter_context(tc.psum_pool(name="psum", bufs=1))
+
+        offs_t = keep.tile([P, S // LANES], U16, name="offs_t")
+        slot_t = keep.tile([P, S // LANES], U16, name="slot_t")
+        xs_all = keep.tile([P, T], U8, name="xs_all", align_bytes=64)
+        xw_all = [keep.tile([P, T], U32, name="xw_all%d" % o, align_bytes=64) for o in range(PASSES)]
+        w_raw = [keep.tile([P, PACK, N], F32, name="w_raw%d" % o, align_bytes=64) for o in range(PASSES)]
+        scale_t = keep.tile([P, S], F32, name="scale_t", align_bytes=64)
+        page = [keep.tile([P, U], F32, name="page%d" % t, align_bytes=64) for t in range(PACK)]
+
+        cache_rows = cache.rearrange("(p t) c -> p t c", t=PACK)
+        out_rows = out_0.rearrange("(p t) c -> p t c", t=PACK)
+
+        nc.vector.memset(xs_all[:].bitcast(I32), 0)
+        nc.sync.dma_start(offs_t[:], offs)
+
+        def load_w(o):
+            nc.sync.dma_start(out=w_raw[o][:], in_=w1[o * K_PASS : (o + 1) * K_PASS, :].rearrange("(p j) c -> p j c", j=PACK))
+
+        def load_x(o):
+            nc.sync.dma_start(out=xw_all[o][:].bitcast(I32), in_=x_words[o].rearrange("p c r -> p (c r)").bitcast(I32))
+
+        load_w(0)
+        for q in range(4):
+            nc.sync.dma_start(
+                out=xs_all[32 * q : 32 * q + 4 * PASSES, :].bitcast(I32),
+                in_=x_scales[:, 4 * q : 4 * q + 4, :].bitcast(I32),
+            )
+        load_x(0)
+        load_w(1)
+        load_x(1)
+        nc.sync.dma_start(out=scale_t[:], in_=scale)
+        nc.sync.dma_start(slot_t[:], slot)
+        for t in (0, 2, 1, 3):
+            nc.sync.dma_start(out=page[t][:], in_=cache_rows[:, t, :])
+
+        xs_got = keep.tile([P, S], U8, name="xs_got", align_bytes=64)
+        xw_got = [keep.tile([P, S], U32, name="xw_got%d" % o, align_bytes=64) for o in range(PASSES)]
+        w_bf = [keep.tile([P, PACK * N], BF16, name="w_bf%d" % o, align_bytes=64) for o in range(PASSES)]
+        w_codes = [keep.tile([P, N], U32, name="w_codes%d" % o, align_bytes=64) for o in range(PASSES)]
+        w_sc = [keep.tile([P, N], U8, name="w_sc%d" % o, align_bytes=64) for o in range(PASSES)]
+        acc = [[psum.tile([P, HALF], F32, name="acc%d%d" % (t, h)) for h in range(2)] for t in range(PACK)]
+        res_scalar = {t: keep.tile([P, S], F32, name="res%d" % t, align_bytes=64) for t in (0, 1, 3)}
+        res_vector = keep.tile([P, S + LAST_VECTOR], F32, name="res_vector", tag="shared", align_bytes=64)
+
+        def res(t, a, b):
+            if t == 2:
+                return res_vector[:, a:b]
+            if t == 3 and b <= LAST_VECTOR:
+                return res_vector[:, S + a : S + b]
+            return res_scalar[t][:, a:b]
+
+        def w_views(o, m0, m1):
+            dst = w_bf[o][:].rearrange("p (t m j) -> p m t j", t=PACK, j=PACK)[:, m0:m1]
+            src = w_raw[o][:].rearrange("p j (m t) -> p m t j", t=PACK)[:, m0:m1]
+            return dst, src
+
+        def quant_w(o, c0, c1):
+            nc.vector.quantize_mx(
+                out=w_codes[o][:, c0:c1].bitcast(FP8X4),
+                scales=w_sc[o][:, c0:c1],
+                in_=w_bf[o][:, PACK * c0 : PACK * c1],
+            )
+
+        def gather_words(o, a, b):
+            nc.vector.tensor_copy(xw_got[o][:, a:b], xw_all[o][:].indirect(offs_t[:, a // LANES : b // LANES]))
+
+        def product(o, t, h):
+            cols = slice(h * HALF, (h + 1) * HALF)
+            rows = slice(t * P, (t + 1) * P)
+            nc.tensor.matmul_mx(
+                out=acc[t][h][:],
+                lhsT=w_codes[o][:, rows].bitcast(FP8X4),
+                lhsT_scale=w_sc[o][:, rows],
+                rhs=xw_got[o][:, cols].bitcast(FP8X4),
+                rhs_scale=xs_got[4 * o : P, cols],
+                start=(o == 0),
+                stop=(o == PASSES - 1),
+            )
+
+        def evacuate(t, a, b):
+            h = a // HALF
+            nc.vector.tensor_tensor(res(t, a, b), acc[t][h][:, a - h * HALF : b - h * HALF], scale_t[:, a:b], MULT)
+
+        def scatter_scalar(t, a, b):
+            nc.scalar.activation(page[t][:].indirect(slot_t[:, a // LANES : b // LANES]), res(t, a, b), COPY)
+
+        def scatter_vector(t, a, b):
+            nc.vector.tensor_copy(page[t][:].indirect(slot_t[:, a // LANES : b // LANES]), res(t, a, b))
+
+        nc.vector.tensor_copy(xs_got[:], xs_all[:].indirect(offs_t[:]))
+        dst, src = w_views(0, 0, P)
+        nc.scalar.activation(dst, src, COPY)
+        gather_words(0, 0, S)
+        quant_w(0, 0, N)
+        for t in range(PACK):
+            for h in range(2):
+                product(0, t, h)
+
+        dst, src = w_views(1, 0, M_VECTOR)
+        nc.vector.tensor_copy(dst, src)
+        dst, src = w_views(1, M_VECTOR, P)
+        nc.scalar.activation(dst, src, COPY)
+        quant_w(1, 0, N // 2)
+        quant_w(1, N // 2, N)
+        gather_words(1, 0, HALF)
+        gather_words(1, HALF, S)
+        for t, h in ((0, 0), (1, 0), (0, 1), (1, 1), (2, 0), (2, 1), (3, 0), (3, 1)):
+            product(1, t, h)
+
+        woven = keep.tile([P, U * PACK], BF16, name="woven", align_bytes=64)
+        o_codes = keep.tile([P, U], U32, name="o_codes", align_bytes=64)
+        o_sc = keep.tile([P, U], U8, name="o_sc", align_bytes=64)
+
+        def round_plane(t, a, b):
+            nc.vector.tensor_copy(pairs_v[:, t // 2, a:b, t % 2], page[t][:, a:b])
+
+        def weave_views(a, b, word):
+            dst = woven[:].bitcast(word).rearrange("p (c u) -> p c u", u=2)[:, a:b]
+            src = pairs[:].bitcast(word).rearrange("p (u c) -> p c u", u=2)[:, a:b]
+            return dst, src
+
+        def store_page(t):
+            nc.sync.dma_start(out=out_rows[:, t, :], in_=page[t][:])
+
+        evacuate(0, 0, HALF)
+        scatter_scalar(0, 0, HALF)
+        evacuate(0, HALF, S)
+        scatter_scalar(0, HALF, S)
+        store_page(0)
+        for t in (1, 2):
+            for h in range(2):
+                evacuate(t, h * HALF, (h + 1) * HALF)
+        scatter_vector(2, 0, S)
+        store_page(2)
+        scatter_scalar(1, 0, HALF)
+        scatter_scalar(1, HALF, S)
+        store_page(1)
+        evacuate(3, 0, LAST_VECTOR)
+        evacuate(3, LAST_VECTOR, HALF)
+        evacuate(3, HALF, S)
+        scatter_vector(3, 0, LAST_VECTOR)
+        scatter_scalar(3, LAST_VECTOR, S)
+        store_page(3)
+        pairs = keep.tile([P, 2 * U * 2], BF16, name="pairs", tag="shared", align_bytes=64)
+        pairs_v = pairs[:].rearrange("p (u c e) -> p u c e", u=2, e=2)
+        for t in (0, 2, 1):
+            round_plane(t, 0, U)
+
+        half_u = U // 2
+        round_plane(3, half_u, U)
+        round_plane(3, 0, half_u)
+        dst, src = weave_views(half_u, U, F32)
+        nc.scalar.copy(dst, src)
+        dst, src = weave_views(0, half_u, F32)
+        nc.vector.tensor_copy(dst, src)
+        words_out = out_1[0].rearrange("p c r -> p (c r)").bitcast(I32)
+        for a in (0, half_u):
+            cols = slice(a, a + half_u)
+            nc.vector.quantize_mx(
+                out=o_codes[:, cols].bitcast(FP8X4),
+                scales=o_sc[:, cols],
+                in_=woven[:, PACK * a : PACK * (a + half_u)],
+            )
+            nc.sync.dma_start(out=words_out[:, cols], in_=o_codes[:, cols].bitcast(I32))
+        for q in range(4):
+            queue = nc.scalar if q % 2 else nc.sync
+            queue.dma_start(out=out_2[0, 4 * q : 4 * q + 4, :].bitcast(I32), in_=o_sc[32 * q : 32 * q + 4, :].bitcast(I32))

@@ -21,14 +21,17 @@ K_PASS = P * PACK
 PASSES = K // K_PASS
 HALF = S // 2
 LANES = 16
-M_VECTOR = 80
 LAST_VECTOR = 128
+HALF_U = U // 2
+QUARTER_U = U // 4
+PAIR_BYTES = 2 * HALF_U * 4
 
 
 def tile_picked_zkvw_none_po_kernel(tc, x_words, x_scales, cache, w1, scale, offs, slot, out_0, out_1, out_2):
     nc = tc.nc
     with ExitStack() as ctx:
         keep = ctx.enter_context(tc.tile_pool(name="keep", bufs=1))
+        reuse = ctx.enter_context(tc.tile_pool(name="reuse", bufs=1))
         psum = ctx.enter_context(tc.psum_pool(name="psum", bufs=1))
 
         offs_t = keep.tile([P, S // LANES], U16, name="offs_t")
@@ -51,15 +54,15 @@ def tile_picked_zkvw_none_po_kernel(tc, x_words, x_scales, cache, w1, scale, off
         def load_x(o):
             nc.sync.dma_start(out=xw_all[o][:].bitcast(I32), in_=x_words[o].rearrange("p c r -> p (c r)").bitcast(I32))
 
-        load_w(0)
+        load_x(0)
         for q in range(4):
             nc.sync.dma_start(
                 out=xs_all[32 * q : 32 * q + 4 * PASSES, :].bitcast(I32),
                 in_=x_scales[:, 4 * q : 4 * q + 4, :].bitcast(I32),
             )
-        load_x(0)
-        load_w(1)
+        load_w(0)
         load_x(1)
+        load_w(1)
         nc.sync.dma_start(out=scale_t[:], in_=scale)
         nc.sync.dma_start(slot_t[:], slot)
         for t in (0, 2, 1, 3):
@@ -67,12 +70,13 @@ def tile_picked_zkvw_none_po_kernel(tc, x_words, x_scales, cache, w1, scale, off
 
         xs_got = keep.tile([P, S], U8, name="xs_got", align_bytes=64)
         xw_got = [keep.tile([P, S], U32, name="xw_got%d" % o, align_bytes=64) for o in range(PASSES)]
-        w_bf = [keep.tile([P, PACK * N], BF16, name="w_bf%d" % o, align_bytes=64) for o in range(PASSES)]
-        w_codes = [keep.tile([P, N], U32, name="w_codes%d" % o, align_bytes=64) for o in range(PASSES)]
-        w_sc = [keep.tile([P, N], U8, name="w_sc%d" % o, align_bytes=64) for o in range(PASSES)]
-        acc = [[psum.tile([P, HALF], F32, name="acc%d%d" % (t, h)) for h in range(2)] for t in range(PACK)]
+        w_bf = [[keep.tile([P, PACK * 2 * P], BF16, name="w_bf%d%d" % (o, u), align_bytes=64) for u in range(2)] for o in range(PASSES)]
+        w_codes = [[keep.tile([P, 2 * P], U32, name="w_codes%d%d" % (o, u), align_bytes=64) for u in range(2)] for o in range(PASSES)]
+        w_sc = [[keep.tile([P, 2 * P], U8, name="w_sc%d%d" % (o, u), align_bytes=64) for u in range(2)] for o in range(PASSES)]
+        groups = [(0, 0, HALF), (0, HALF, S), (1, 0, S), (2, 0, S), (3, 0, S)]
+        acc = {(t, a): psum.tile([P, b - a], F32, name="acc%d_%d" % (t, a)) for t, a, b in groups}
         res_scalar = {t: keep.tile([P, S], F32, name="res%d" % t, align_bytes=64) for t in (0, 1, 3)}
-        res_vector = keep.tile([P, S + LAST_VECTOR], F32, name="res_vector", tag="shared", align_bytes=64)
+        res_vector = reuse.tile([P, S + LAST_VECTOR], F32, name="res_vector", offset=PAIR_BYTES - 1280)
 
         def res(t, a, b):
             if t == 2:
@@ -81,28 +85,24 @@ def tile_picked_zkvw_none_po_kernel(tc, x_words, x_scales, cache, w1, scale, off
                 return res_vector[:, S + a : S + b]
             return res_scalar[t][:, a:b]
 
-        def w_views(o, m0, m1):
-            dst = w_bf[o][:].rearrange("p (t m j) -> p m t j", t=PACK, j=PACK)[:, m0:m1]
-            src = w_raw[o][:].rearrange("p j (m t) -> p m t j", t=PACK)[:, m0:m1]
+        def w_views(o, u):
+            dst = w_bf[o][u][:].rearrange("p (e m j) -> p m e j", e=2, j=PACK)
+            src = w_raw[o][:].rearrange("p j (m u e) -> p u m e j", u=2, e=2)[:, u]
             return dst, src
 
-        def quant_w(o, c0, c1):
-            nc.vector.quantize_mx(
-                out=w_codes[o][:, c0:c1].bitcast(FP8X4),
-                scales=w_sc[o][:, c0:c1],
-                in_=w_bf[o][:, PACK * c0 : PACK * c1],
-            )
+        def quant_w(o, u):
+            nc.vector.quantize_mx(out=w_codes[o][u][:].bitcast(FP8X4), scales=w_sc[o][u][:], in_=w_bf[o][u][:])
 
         def gather_words(o, a, b):
             nc.vector.tensor_copy(xw_got[o][:, a:b], xw_all[o][:].indirect(offs_t[:, a // LANES : b // LANES]))
 
-        def product(o, t, h):
-            cols = slice(h * HALF, (h + 1) * HALF)
-            rows = slice(t * P, (t + 1) * P)
+        def product(o, t, a, b):
+            cols = slice(a, b)
+            rows = slice(t % 2 * P, (t % 2 + 1) * P)
             nc.tensor.matmul_mx(
-                out=acc[t][h][:],
-                lhsT=w_codes[o][:, rows].bitcast(FP8X4),
-                lhsT_scale=w_sc[o][:, rows],
+                out=acc[(t, a)][:],
+                lhsT=w_codes[o][t // 2][:, rows].bitcast(FP8X4),
+                lhsT_scale=w_sc[o][t // 2][:, rows],
                 rhs=xw_got[o][:, cols].bitcast(FP8X4),
                 rhs_scale=xs_got[4 * o : P, cols],
                 start=(o == 0),
@@ -110,8 +110,8 @@ def tile_picked_zkvw_none_po_kernel(tc, x_words, x_scales, cache, w1, scale, off
             )
 
         def evacuate(t, a, b):
-            h = a // HALF
-            nc.vector.tensor_tensor(res(t, a, b), acc[t][h][:, a - h * HALF : b - h * HALF], scale_t[:, a:b], MULT)
+            first = max(g[1] for g in groups if g[0] == t and g[1] <= a)
+            nc.vector.tensor_tensor(res(t, a, b), acc[(t, first)][:, a - first : b - first], scale_t[:, a:b], MULT)
 
         def scatter_scalar(t, a, b):
             nc.scalar.activation(page[t][:].indirect(slot_t[:, a // LANES : b // LANES]), res(t, a, b), COPY)
@@ -119,36 +119,33 @@ def tile_picked_zkvw_none_po_kernel(tc, x_words, x_scales, cache, w1, scale, off
         def scatter_vector(t, a, b):
             nc.vector.tensor_copy(page[t][:].indirect(slot_t[:, a // LANES : b // LANES]), res(t, a, b))
 
-        nc.vector.tensor_copy(xs_got[:], xs_all[:].indirect(offs_t[:]))
-        dst, src = w_views(0, 0, P)
-        nc.scalar.activation(dst, src, COPY)
-        gather_words(0, 0, S)
-        quant_w(0, 0, N)
-        for t in range(PACK):
-            for h in range(2):
-                product(0, t, h)
+        for o in range(PASSES):
+            gather_words(o, 0, S)
+            if o == 0:
+                nc.vector.tensor_copy(xs_got[:], xs_all[:].indirect(offs_t[:]))
+            dst, src = w_views(o, 0)
+            nc.vector.tensor_copy(dst, src)
+            dst, src = w_views(o, 1)
+            nc.scalar.activation(dst, src, COPY)
+            for u in range(2):
+                quant_w(o, u)
+                for t, a, b in groups:
+                    if t // 2 == u:
+                        product(o, t, a, b)
 
-        dst, src = w_views(1, 0, M_VECTOR)
-        nc.vector.tensor_copy(dst, src)
-        dst, src = w_views(1, M_VECTOR, P)
-        nc.scalar.activation(dst, src, COPY)
-        quant_w(1, 0, N // 2)
-        quant_w(1, N // 2, N)
-        gather_words(1, 0, HALF)
-        gather_words(1, HALF, S)
-        for t, h in ((0, 0), (1, 0), (0, 1), (1, 1), (2, 0), (2, 1), (3, 0), (3, 1)):
-            product(1, t, h)
-
-        woven = keep.tile([P, U * PACK], BF16, name="woven", align_bytes=64)
+        pieces = ((HALF_U, HALF_U + QUARTER_U), (0, HALF_U), (HALF_U + QUARTER_U, U))
+        woven = {a: keep.tile([P, (b - a) * PACK], BF16, name="woven%d" % a, align_bytes=64) for a, b in pieces}
         o_codes = keep.tile([P, U], U32, name="o_codes", align_bytes=64)
         o_sc = keep.tile([P, U], U8, name="o_sc", align_bytes=64)
 
-        def round_plane(t, a, b):
-            nc.vector.tensor_copy(pairs_v[:, t // 2, a:b, t % 2], page[t][:, a:b])
+        def round_plane(t, v):
+            dst = pairs[v][:].rearrange("p (u c e) -> p u c e", u=2, e=2)[:, t // 2, :, t % 2]
+            nc.vector.tensor_copy(dst, page[t][:, v * HALF_U : (v + 1) * HALF_U])
 
-        def weave_views(a, b, word):
-            dst = woven[:].bitcast(word).rearrange("p (c u) -> p c u", u=2)[:, a:b]
-            src = pairs[:].bitcast(word).rearrange("p (u c) -> p c u", u=2)[:, a:b]
+        def weave_views(a, b):
+            v = a // HALF_U
+            dst = woven[a][:].bitcast(F32).rearrange("p (c u) -> p c u", u=2)
+            src = pairs[v][:].bitcast(F32).rearrange("p (u c) -> p c u", u=2)[:, a - v * HALF_U : b - v * HALF_U]
             return dst, src
 
         def store_page(t):
@@ -160,39 +157,32 @@ def tile_picked_zkvw_none_po_kernel(tc, x_words, x_scales, cache, w1, scale, off
         scatter_scalar(0, HALF, S)
         store_page(0)
         for t in (1, 2):
-            for h in range(2):
-                evacuate(t, h * HALF, (h + 1) * HALF)
+            evacuate(t, 0, S)
         scatter_vector(2, 0, S)
         store_page(2)
         scatter_scalar(1, 0, HALF)
         scatter_scalar(1, HALF, S)
         store_page(1)
         evacuate(3, 0, LAST_VECTOR)
-        evacuate(3, LAST_VECTOR, HALF)
-        evacuate(3, HALF, S)
+        evacuate(3, LAST_VECTOR, S)
         scatter_vector(3, 0, LAST_VECTOR)
         scatter_scalar(3, LAST_VECTOR, S)
         store_page(3)
-        pairs = keep.tile([P, 2 * U * 2], BF16, name="pairs", tag="shared", align_bytes=64)
-        pairs_v = pairs[:].rearrange("p (u c e) -> p u c e", u=2, e=2)
-        for t in (0, 2, 1):
-            round_plane(t, 0, U)
+        pairs = [reuse.tile([P, 2 * HALF_U * 2], BF16, name="pairs%d" % v, offset=v * PAIR_BYTES) for v in range(2)]
+        for t in (0, 2, 1, 3):
+            for v in (1, 0):
+                round_plane(t, v)
 
-        half_u = U // 2
-        round_plane(3, half_u, U)
-        round_plane(3, 0, half_u)
-        dst, src = weave_views(half_u, U, F32)
-        nc.scalar.copy(dst, src)
-        dst, src = weave_views(0, half_u, F32)
-        nc.vector.tensor_copy(dst, src)
+        for a, b in pieces:
+            dst, src = weave_views(a, b)
+            if a >= HALF_U:
+                nc.scalar.copy(dst, src)
+            else:
+                nc.vector.tensor_copy(dst, src)
         words_out = out_1[0].rearrange("p c r -> p (c r)").bitcast(I32)
-        for a in (0, half_u):
-            cols = slice(a, a + half_u)
-            nc.vector.quantize_mx(
-                out=o_codes[:, cols].bitcast(FP8X4),
-                scales=o_sc[:, cols],
-                in_=woven[:, PACK * a : PACK * (a + half_u)],
-            )
+        for a, b in pieces:
+            cols = slice(a, b)
+            nc.vector.quantize_mx(out=o_codes[:, cols].bitcast(FP8X4), scales=o_sc[:, cols], in_=woven[a][:])
             nc.sync.dma_start(out=words_out[:, cols], in_=o_codes[:, cols].bitcast(I32))
         for q in range(4):
             queue = nc.scalar if q % 2 else nc.sync

@@ -1,6 +1,7 @@
 from contextlib import ExitStack
 
 import concourse.mybir as mybir
+from concourse.masks import make_identity
 
 K, T, S, N, U = 1024, 1024, 512, 512, 1024
 FLOPS = 2 * K * N * S
@@ -14,6 +15,7 @@ U8 = mybir.dt.uint8
 FP8X4 = mybir.dt.float8_e4m3fn_x4
 COPY = mybir.ActivationFunctionType.Copy
 MULT = mybir.AluOpType.mult
+ADD = mybir.AluOpType.add
 
 P = 128
 PACK = 4
@@ -21,17 +23,15 @@ K_PASS = P * PACK
 PASSES = K // K_PASS
 HALF = S // 2
 LANES = 16
-LAST_VECTOR = 128
-HALF_U = U // 2
-QUARTER_U = U // 4
-PAIR_BYTES = 2 * HALF_U * 4
+SHARED_SCALAR = 128
+LAST_FIRST = 128
+PIECES = ((0, 256), (256, 640), (640, U))
 
 
 def tile_picked_zkvw_none_po_kernel(tc, x_words, x_scales, cache, w1, scale, offs, slot, out_0, out_1, out_2):
     nc = tc.nc
     with ExitStack() as ctx:
         keep = ctx.enter_context(tc.tile_pool(name="keep", bufs=1))
-        reuse = ctx.enter_context(tc.tile_pool(name="reuse", bufs=1))
         psum = ctx.enter_context(tc.psum_pool(name="psum", bufs=1))
 
         offs_t = keep.tile([P, S // LANES], U16, name="offs_t")
@@ -47,6 +47,14 @@ def tile_picked_zkvw_none_po_kernel(tc, x_words, x_scales, cache, w1, scale, off
 
         nc.vector.memset(xs_all[:].bitcast(I32), 0)
         nc.sync.dma_start(offs_t[:], offs)
+        scale_col = keep.tile([P, PACK], F32, name="scale_col")
+        nc.sync.dma_start(out=scale_col[:], in_=scale[0].rearrange("(p i) -> p i", i=PACK))
+        ident = keep.tile([P, P], F32, name="ident")
+        make_identity(nc, ident[:])
+        spread = psum.tile([P, PACK, P], F32, name="spread")
+        for i in range(PACK):
+            nc.tensor.transpose(spread[:, i, :], scale_col[:, i : i + 1].to_broadcast([P, P]), ident[:])
+        nc.scalar.activation(scale_t[:].rearrange("q (p i) -> q p i", i=PACK), spread[:].rearrange("q i p -> q p i"), COPY)
 
         def load_w(o):
             nc.sync.dma_start(out=w_raw[o][:], in_=w1[o * K_PASS : (o + 1) * K_PASS, :].rearrange("(p j) c -> p j c", j=PACK))
@@ -63,9 +71,8 @@ def tile_picked_zkvw_none_po_kernel(tc, x_words, x_scales, cache, w1, scale, off
         load_w(0)
         load_x(1)
         load_w(1)
-        nc.sync.dma_start(out=scale_t[:], in_=scale)
         nc.sync.dma_start(slot_t[:], slot)
-        for t in (0, 2, 1, 3):
+        for t in range(PACK):
             nc.sync.dma_start(out=page[t][:], in_=cache_rows[:, t, :])
 
         xs_got = keep.tile([P, S], U8, name="xs_got", align_bytes=64)
@@ -73,21 +80,13 @@ def tile_picked_zkvw_none_po_kernel(tc, x_words, x_scales, cache, w1, scale, off
         w_bf = [[keep.tile([P, PACK * 2 * P], BF16, name="w_bf%d%d" % (o, u), align_bytes=64) for u in range(2)] for o in range(PASSES)]
         w_codes = [[keep.tile([P, 2 * P], U32, name="w_codes%d%d" % (o, u), align_bytes=64) for u in range(2)] for o in range(PASSES)]
         w_sc = [[keep.tile([P, 2 * P], U8, name="w_sc%d%d" % (o, u), align_bytes=64) for u in range(2)] for o in range(PASSES)]
-        groups = [(0, 0, HALF), (0, HALF, S), (1, 0, S), (2, 0, S), (3, 0, S)]
+        groups = [(0, 0, HALF), (0, HALF, S), (2, 0, S), (3, 0, S), (1, 0, S)]
         acc = {(t, a): psum.tile([P, b - a], F32, name="acc%d_%d" % (t, a)) for t, a, b in groups}
-        res_scalar = {t: keep.tile([P, S], F32, name="res%d" % t, align_bytes=64) for t in (0, 1, 3)}
-        res_vector = reuse.tile([P, S + LAST_VECTOR], F32, name="res_vector", offset=PAIR_BYTES - 1280)
-
-        def res(t, a, b):
-            if t == 2:
-                return res_vector[:, a:b]
-            if t == 3 and b <= LAST_VECTOR:
-                return res_vector[:, S + a : S + b]
-            return res_scalar[t][:, a:b]
+        res = {}
 
         def w_views(o, u):
             dst = w_bf[o][u][:].rearrange("p (e m j) -> p m e j", e=2, j=PACK)
-            src = w_raw[o][:].rearrange("p j (m u e) -> p u m e j", u=2, e=2)[:, u]
+            src = w_raw[o][:].rearrange("p j (m e u) -> p u m e j", u=2, e=2)[:, u]
             return dst, src
 
         def quant_w(o, u):
@@ -98,26 +97,29 @@ def tile_picked_zkvw_none_po_kernel(tc, x_words, x_scales, cache, w1, scale, off
 
         def product(o, t, a, b):
             cols = slice(a, b)
-            rows = slice(t % 2 * P, (t % 2 + 1) * P)
+            rows = slice(t // 2 * P, (t // 2 + 1) * P)
             nc.tensor.matmul_mx(
                 out=acc[(t, a)][:],
-                lhsT=w_codes[o][t // 2][:, rows].bitcast(FP8X4),
-                lhsT_scale=w_sc[o][t // 2][:, rows],
+                lhsT=w_codes[o][t % 2][:, rows].bitcast(FP8X4),
+                lhsT_scale=w_sc[o][t % 2][:, rows],
                 rhs=xw_got[o][:, cols].bitcast(FP8X4),
                 rhs_scale=xs_got[4 * o : P, cols],
                 start=(o == 0),
                 stop=(o == PASSES - 1),
             )
 
-        def evacuate(t, a, b):
+        def evacuate(t, a, b, place=None):
             first = max(g[1] for g in groups if g[0] == t and g[1] <= a)
-            nc.vector.tensor_tensor(res(t, a, b), acc[(t, first)][:, a - first : b - first], scale_t[:, a:b], MULT)
+            if place is None:
+                place = keep.tile([P, b - a], F32, name="res%d_%d" % (t, a), align_bytes=64)[:]
+            res[(t, a)] = place
+            nc.vector.tensor_tensor(place, acc[(t, first)][:, a - first : b - first], scale_t[:, a:b], MULT)
 
-        def scatter_scalar(t, a, b):
-            nc.scalar.activation(page[t][:].indirect(slot_t[:, a // LANES : b // LANES]), res(t, a, b), COPY)
+        def scatter_scalar(t, a, b, source):
+            nc.scalar.activation(page[t][:].indirect(slot_t[:, a // LANES : b // LANES]), source, COPY)
 
-        def scatter_vector(t, a, b):
-            nc.vector.tensor_copy(page[t][:].indirect(slot_t[:, a // LANES : b // LANES]), res(t, a, b))
+        def scatter_vector(t, a, b, source):
+            nc.vector.tensor_copy(page[t][:].indirect(slot_t[:, a // LANES : b // LANES]), source)
 
         for o in range(PASSES):
             gather_words(o, 0, S)
@@ -130,57 +132,59 @@ def tile_picked_zkvw_none_po_kernel(tc, x_words, x_scales, cache, w1, scale, off
             for u in range(2):
                 quant_w(o, u)
                 for t, a, b in groups:
-                    if t // 2 == u:
+                    if t % 2 == u:
                         product(o, t, a, b)
 
-        pieces = ((HALF_U, HALF_U + QUARTER_U), (0, HALF_U), (HALF_U + QUARTER_U, U))
-        woven = {a: keep.tile([P, (b - a) * PACK], BF16, name="woven%d" % a, align_bytes=64) for a, b in pieces}
+        pairs = {a: keep.tile([P, (b - a) * PACK], BF16, name="pairs%d" % a, align_bytes=64) for a, b in PIECES}
+        woven = {a: keep.tile([P, (b - a) * PACK], BF16, name="woven%d" % a, align_bytes=64) for a, b in PIECES}
         o_codes = keep.tile([P, U], U32, name="o_codes", align_bytes=64)
         o_sc = keep.tile([P, U], U8, name="o_sc", align_bytes=64)
 
-        def round_plane(t, v):
-            dst = pairs[v][:].rearrange("p (u c e) -> p u c e", u=2, e=2)[:, t // 2, :, t % 2]
-            nc.vector.tensor_copy(dst, page[t][:, v * HALF_U : (v + 1) * HALF_U])
+        def pair_view(t, a):
+            return pairs[a][:].rearrange("p (u c e) -> p u c e", u=2, e=2)[:, t // 2, :, t % 2]
 
-        def weave_views(a, b):
-            v = a // HALF_U
+        def weave_views(a):
             dst = woven[a][:].bitcast(F32).rearrange("p (c u) -> p c u", u=2)
-            src = pairs[v][:].bitcast(F32).rearrange("p (u c) -> p c u", u=2)[:, a - v * HALF_U : b - v * HALF_U]
+            src = pairs[a][:].bitcast(F32).rearrange("p (u c) -> p c u", u=2)
             return dst, src
 
         def store_page(t):
             nc.sync.dma_start(out=out_rows[:, t, :], in_=page[t][:])
 
         evacuate(0, 0, HALF)
-        scatter_scalar(0, 0, HALF)
         evacuate(0, HALF, S)
-        scatter_scalar(0, HALF, S)
+        evacuate(2, 0, S)
+        evacuate(3, 0, LAST_FIRST)
+        evacuate(3, LAST_FIRST, S, pairs[PIECES[2][0]][:].bitcast(F32)[:, S - LAST_FIRST :])
+        evacuate(1, 0, S)
+        scatter_scalar(0, 0, HALF, res[(0, 0)])
+        scatter_scalar(0, HALF, S, res[(0, HALF)])
         store_page(0)
-        for t in (1, 2):
-            evacuate(t, 0, S)
-        scatter_vector(2, 0, S)
-        store_page(2)
-        scatter_scalar(1, 0, HALF)
-        scatter_scalar(1, HALF, S)
+        scatter_vector(1, 0, S, res[(1, 0)])
         store_page(1)
-        evacuate(3, 0, LAST_VECTOR)
-        evacuate(3, LAST_VECTOR, S)
-        scatter_vector(3, 0, LAST_VECTOR)
-        scatter_scalar(3, LAST_VECTOR, S)
+        scatter_scalar(2, 0, SHARED_SCALAR, res[(2, 0)][:, 0:SHARED_SCALAR])
+        scatter_scalar(3, 0, LAST_FIRST, res[(3, 0)])
+        scatter_scalar(3, LAST_FIRST, S, res[(3, LAST_FIRST)])
+        scatter_vector(2, SHARED_SCALAR, S, res[(2, 0)][:, SHARED_SCALAR:S])
+        store_page(2)
         store_page(3)
-        pairs = [reuse.tile([P, 2 * HALF_U * 2], BF16, name="pairs%d" % v, offset=v * PAIR_BYTES) for v in range(2)]
-        for t in (0, 2, 1, 3):
-            for v in (1, 0):
-                round_plane(t, v)
+        for t in (0, 1):
+            for a, b in PIECES:
+                nc.gpsimd.tensor_scalar(pair_view(t, a), page[t][:, a:b], 1.0, 0.0, MULT, ADD)
 
-        for a, b in pieces:
-            dst, src = weave_views(a, b)
-            if a >= HALF_U:
-                nc.scalar.copy(dst, src)
-            else:
-                nc.vector.tensor_copy(dst, src)
+        for t in (2, 3):
+            for a, b in PIECES[:2]:
+                nc.vector.tensor_copy(pair_view(t, a), page[t][:, a:b])
+        a, b = PIECES[2]
+        for t in (3, 2):
+            nc.scalar.copy(pair_view(t, a), page[t][:, a:b])
+        dst, src = weave_views(a)
+        nc.scalar.copy(dst, src)
+        for a, b in PIECES[:2]:
+            dst, src = weave_views(a)
+            nc.vector.tensor_copy(dst, src)
         words_out = out_1[0].rearrange("p c r -> p (c r)").bitcast(I32)
-        for a, b in pieces:
+        for a, b in PIECES:
             cols = slice(a, b)
             nc.vector.quantize_mx(out=o_codes[:, cols].bitcast(FP8X4), scales=o_sc[:, cols], in_=woven[a][:])
             nc.sync.dma_start(out=words_out[:, cols], in_=o_codes[:, cols].bitcast(I32))

@@ -46,23 +46,18 @@ def tile_picked_zkvw_none_po_kernel(tc, x_words, x_scales, cache, w1, scale, off
         out_rows = out_0.rearrange("(p t) c -> p t c", t=PACK)
 
         nc.vector.memset(xs_all[:].bitcast(I32), 0)
-        nc.sync.dma_start(offs_t[:], offs)
-        scale_col = keep.tile([P, PACK], F32, name="scale_col")
-        nc.sync.dma_start(out=scale_col[:], in_=scale[0].rearrange("(p i) -> p i", i=PACK))
-        ident = keep.tile([P, P], F32, name="ident")
-        make_identity(nc, ident[:])
-        spread = psum.tile([P, PACK, P], F32, name="spread")
-        for i in range(PACK):
-            nc.tensor.transpose(spread[:, i, :], scale_col[:, i : i + 1].to_broadcast([P, P]), ident[:])
-        nc.scalar.activation(scale_t[:].rearrange("q (p i) -> q p i", i=PACK), spread[:].rearrange("q i p -> q p i"), COPY)
 
         def load_w(o):
-            nc.sync.dma_start(out=w_raw[o][:], in_=w1[o * K_PASS : (o + 1) * K_PASS, :].rearrange("(p j) c -> p j c", j=PACK))
+            rows = w1[o * K_PASS : (o + 1) * K_PASS, :].rearrange("(p j) c -> p j c", j=PACK)
+            nc.sync.dma_start(out=w_raw[o][:], in_=rows)
 
         def load_x(o):
             nc.sync.dma_start(out=xw_all[o][:].bitcast(I32), in_=x_words[o].rearrange("p c r -> p (c r)").bitcast(I32))
 
         load_x(0)
+        nc.sync.dma_start(offs_t[:], offs)
+        scale_col = keep.tile([P, PACK], F32, name="scale_col")
+        nc.sync.dma_start(out=scale_col[:], in_=scale[0].rearrange("(p i) -> p i", i=PACK))
         for q in range(4):
             nc.sync.dma_start(
                 out=xs_all[32 * q : 32 * q + 4 * PASSES, :].bitcast(I32),
@@ -75,6 +70,13 @@ def tile_picked_zkvw_none_po_kernel(tc, x_words, x_scales, cache, w1, scale, off
         for t in range(PACK):
             nc.sync.dma_start(out=page[t][:], in_=cache_rows[:, t, :])
 
+        ident = keep.tile([P, P], F32, name="ident")
+        make_identity(nc, ident[:])
+        spread = psum.tile([P, PACK, P], F32, name="spread")
+        for i in range(PACK):
+            nc.tensor.transpose(spread[:, i, :], scale_col[:, i : i + 1].to_broadcast([P, P]), ident[:])
+        nc.scalar.activation(scale_t[:].rearrange("q (p i) -> q p i", i=PACK), spread[:].rearrange("q i p -> q p i"), COPY)
+
         xs_got = keep.tile([P, S], U8, name="xs_got", align_bytes=64)
         xw_got = [keep.tile([P, S], U32, name="xw_got%d" % o, align_bytes=64) for o in range(PASSES)]
         w_bf = [[keep.tile([P, PACK * 2 * P], BF16, name="w_bf%d%d" % (o, u), align_bytes=64) for u in range(2)] for o in range(PASSES)]
@@ -84,9 +86,9 @@ def tile_picked_zkvw_none_po_kernel(tc, x_words, x_scales, cache, w1, scale, off
         acc = {(t, a): psum.tile([P, b - a], F32, name="acc%d_%d" % (t, a)) for t, a, b in groups}
         res = {}
 
-        def w_views(o, u):
-            dst = w_bf[o][u][:].rearrange("p (e m j) -> p m e j", e=2, j=PACK)
-            src = w_raw[o][:].rearrange("p j (m e u) -> p u m e j", u=2, e=2)[:, u]
+        def w_views(o, u, m0, m1):
+            dst = w_bf[o][u][:].rearrange("p (e m j) -> p m e j", e=2, j=PACK)[:, m0:m1]
+            src = w_raw[o][:].rearrange("p j (m e u) -> p u m e j", u=2, e=2)[:, u, m0:m1]
             return dst, src
 
         def quant_w(o, u):
@@ -125,9 +127,9 @@ def tile_picked_zkvw_none_po_kernel(tc, x_words, x_scales, cache, w1, scale, off
             gather_words(o, 0, S)
             if o == 0:
                 nc.vector.tensor_copy(xs_got[:], xs_all[:].indirect(offs_t[:]))
-            dst, src = w_views(o, 0)
+            dst, src = w_views(o, 0, 0, P)
             nc.vector.tensor_copy(dst, src)
-            dst, src = w_views(o, 1)
+            dst, src = w_views(o, 1, 0, P)
             nc.scalar.activation(dst, src, COPY)
             for u in range(2):
                 quant_w(o, u)

from contextlib import ExitStack

import concourse.mybir as mybir
from concourse.masks import make_identity

K, T, S, N, U = 1024, 1024, 512, 512, 1024
FLOPS = 2 * K * N * S

F32 = mybir.dt.float32
BF16 = mybir.dt.bfloat16
I32 = mybir.dt.int32
U32 = mybir.dt.uint32
U16 = mybir.dt.uint16
U8 = mybir.dt.uint8
FP8X4 = mybir.dt.float8_e4m3fn_x4
COPY = mybir.ActivationFunctionType.Copy
MULT = mybir.AluOpType.mult
ADD = mybir.AluOpType.add

P = 128
PACK = 4
K_PASS = P * PACK
PASSES = K // K_PASS
HALF = S // 2
LANES = 16
SHARED_SCALAR = 128
LAST_FIRST = 128
PIECES = ((0, 256), (256, 640), (640, U))


def tile_picked_zkvw_none_po_kernel(tc, x_words, x_scales, cache, w1, scale, offs, slot, out_0, out_1, out_2):
    nc = tc.nc
    with ExitStack() as ctx:
        keep = ctx.enter_context(tc.tile_pool(name="keep", bufs=1))
        psum = ctx.enter_context(tc.psum_pool(name="psum", bufs=1))

        offs_t = keep.tile([P, S // LANES], U16, name="offs_t")
        slot_t = keep.tile([P, S // LANES], U16, name="slot_t")
        xs_all = keep.tile([P, T], U8, name="xs_all", align_bytes=64)
        xw_all = [keep.tile([P, T], U32, name="xw_all%d" % o, align_bytes=64) for o in range(PASSES)]
        w_raw = [keep.tile([P, PACK, N], F32, name="w_raw%d" % o, align_bytes=64) for o in range(PASSES)]
        scale_t = keep.tile([P, S], F32, name="scale_t", align_bytes=64)
        page = [keep.tile([P, U], F32, name="page%d" % t, align_bytes=64) for t in range(PACK)]

        cache_rows = cache.rearrange("(p t) c -> p t c", t=PACK)
        out_rows = out_0.rearrange("(p t) c -> p t c", t=PACK)

        nc.vector.memset(xs_all[:].bitcast(I32), 0)

        def load_w(o):
            rows = w1[o * K_PASS : (o + 1) * K_PASS, :].rearrange("(p j) c -> p j c", j=PACK)
            nc.sync.dma_start(out=w_raw[o][:], in_=rows)

        def load_x(o):
            nc.sync.dma_start(out=xw_all[o][:].bitcast(I32), in_=x_words[o].rearrange("p c r -> p (c r)").bitcast(I32))

        load_x(0)
        nc.sync.dma_start(offs_t[:], offs)
        scale_col = keep.tile([P, PACK], F32, name="scale_col")
        nc.sync.dma_start(out=scale_col[:], in_=scale[0].rearrange("(p i) -> p i", i=PACK))
        for q in range(4):
            nc.sync.dma_start(
                out=xs_all[32 * q : 32 * q + 4 * PASSES, :].bitcast(I32),
                in_=x_scales[:, 4 * q : 4 * q + 4, :].bitcast(I32),
            )
        load_w(0)
        load_x(1)
        load_w(1)
        nc.sync.dma_start(slot_t[:], slot)
        for t in range(PACK):
            nc.sync.dma_start(out=page[t][:], in_=cache_rows[:, t, :])

        ident = keep.tile([P, P], F32, name="ident")
        make_identity(nc, ident[:])
        spread = psum.tile([P, PACK, P], F32, name="spread")
        for i in range(PACK):
            nc.tensor.transpose(spread[:, i, :], scale_col[:, i : i + 1].to_broadcast([P, P]), ident[:])
        nc.scalar.activation(scale_t[:].rearrange("q (p i) -> q p i", i=PACK), spread[:].rearrange("q i p -> q p i"), COPY)

        xs_got = keep.tile([P, S], U8, name="xs_got", align_bytes=64)
        xw_got = [keep.tile([P, S], U32, name="xw_got%d" % o, align_bytes=64) for o in range(PASSES)]
        w_bf = [[keep.tile([P, PACK * 2 * P], BF16, name="w_bf%d%d" % (o, u), align_bytes=64) for u in range(2)] for o in range(PASSES)]
        w_codes = [[keep.tile([P, 2 * P], U32, name="w_codes%d%d" % (o, u), align_bytes=64) for u in range(2)] for o in range(PASSES)]
        w_sc = [[keep.tile([P, 2 * P], U8, name="w_sc%d%d" % (o, u), align_bytes=64) for u in range(2)] for o in range(PASSES)]
        groups = [(0, 0, HALF), (0, HALF, S), (2, 0, S), (3, 0, S), (1, 0, S)]
        acc = {(t, a): psum.tile([P, b - a], F32, name="acc%d_%d" % (t, a)) for t, a, b in groups}
        res = {}

        def w_views(o, u, m0, m1):
            dst = w_bf[o][u][:].rearrange("p (e m j) -> p m e j", e=2, j=PACK)[:, m0:m1]
            src = w_raw[o][:].rearrange("p j (m e u) -> p u m e j", u=2, e=2)[:, u, m0:m1]
            return dst, src

        def quant_w(o, u):
            nc.vector.quantize_mx(out=w_codes[o][u][:].bitcast(FP8X4), scales=w_sc[o][u][:], in_=w_bf[o][u][:])

        def gather_words(o, a, b):
            nc.vector.tensor_copy(xw_got[o][:, a:b], xw_all[o][:].indirect(offs_t[:, a // LANES : b // LANES]))

        def product(o, t, a, b):
            cols = slice(a, b)
            rows = slice(t // 2 * P, (t // 2 + 1) * P)
            nc.tensor.matmul_mx(
                out=acc[(t, a)][:],
                lhsT=w_codes[o][t % 2][:, rows].bitcast(FP8X4),
                lhsT_scale=w_sc[o][t % 2][:, rows],
                rhs=xw_got[o][:, cols].bitcast(FP8X4),
                rhs_scale=xs_got[4 * o : P, cols],
                start=(o == 0),
                stop=(o == PASSES - 1),
            )

        def evacuate(t, a, b, place=None):
            first = max(g[1] for g in groups if g[0] == t and g[1] <= a)
            if place is None:
                place = keep.tile([P, b - a], F32, name="res%d_%d" % (t, a), align_bytes=64)[:]
            res[(t, a)] = place
            nc.vector.tensor_tensor(place, acc[(t, first)][:, a - first : b - first], scale_t[:, a:b], MULT)

        def scatter_scalar(t, a, b, source):
            nc.scalar.activation(page[t][:].indirect(slot_t[:, a // LANES : b // LANES]), source, COPY)

        def scatter_vector(t, a, b, source):
            nc.vector.tensor_copy(page[t][:].indirect(slot_t[:, a // LANES : b // LANES]), source)

        for o in range(PASSES):
            gather_words(o, 0, S)
            if o == 0:
                nc.vector.tensor_copy(xs_got[:], xs_all[:].indirect(offs_t[:]))
            dst, src = w_views(o, 0, 0, P)
            nc.vector.tensor_copy(dst, src)
            dst, src = w_views(o, 1, 0, P)
            nc.scalar.activation(dst, src, COPY)
            for u in range(2):
                quant_w(o, u)
                for t, a, b in groups:
                    if t % 2 == u:
                        product(o, t, a, b)

        pairs = {a: keep.tile([P, (b - a) * PACK], BF16, name="pairs%d" % a, align_bytes=64) for a, b in PIECES}
        woven = {a: keep.tile([P, (b - a) * PACK], BF16, name="woven%d" % a, align_bytes=64) for a, b in PIECES}
        o_codes = keep.tile([P, U], U32, name="o_codes", align_bytes=64)
        o_sc = keep.tile([P, U], U8, name="o_sc", align_bytes=64)

        def pair_view(t, a):
            return pairs[a][:].rearrange("p (u c e) -> p u c e", u=2, e=2)[:, t // 2, :, t % 2]

        def weave_views(a):
            dst = woven[a][:].bitcast(F32).rearrange("p (c u) -> p c u", u=2)
            src = pairs[a][:].bitcast(F32).rearrange("p (u c) -> p c u", u=2)
            return dst, src

        def store_page(t):
            nc.sync.dma_start(out=out_rows[:, t, :], in_=page[t][:])

        evacuate(0, 0, HALF)
        evacuate(0, HALF, S)
        evacuate(2, 0, S)
        evacuate(3, 0, LAST_FIRST)
        evacuate(3, LAST_FIRST, S, pairs[PIECES[2][0]][:].bitcast(F32)[:, S - LAST_FIRST :])
        evacuate(1, 0, S)
        scatter_scalar(0, 0, HALF, res[(0, 0)])
        scatter_scalar(0, HALF, S, res[(0, HALF)])
        store_page(0)
        scatter_vector(1, 0, S, res[(1, 0)])
        store_page(1)
        scatter_scalar(2, 0, SHARED_SCALAR, res[(2, 0)][:, 0:SHARED_SCALAR])
        scatter_scalar(3, 0, LAST_FIRST, res[(3, 0)])
        scatter_scalar(3, LAST_FIRST, S, res[(3, LAST_FIRST)])
        scatter_vector(2, SHARED_SCALAR, S, res[(2, 0)][:, SHARED_SCALAR:S])
        store_page(2)
        store_page(3)
        for t in (0, 1):
            for a, b in PIECES:
                nc.gpsimd.tensor_scalar(pair_view(t, a), page[t][:, a:b], 1.0, 0.0, MULT, ADD)

        for t in (2, 3):
            for a, b in PIECES[:2]:
                nc.vector.tensor_copy(pair_view(t, a), page[t][:, a:b])
        a, b = PIECES[2]
        for t in (3, 2):
            nc.scalar.copy(pair_view(t, a), page[t][:, a:b])
        dst, src = weave_views(a)
        nc.scalar.copy(dst, src)
        for a, b in PIECES[:2]:
            dst, src = weave_views(a)
            nc.vector.tensor_copy(dst, src)
        words_out = out_1[0].rearrange("p c r -> p (c r)").bitcast(I32)
        for a, b in PIECES:
            cols = slice(a, b)
            nc.vector.quantize_mx(out=o_codes[:, cols].bitcast(FP8X4), scales=o_sc[:, cols], in_=woven[a][:])
            nc.sync.dma_start(out=words_out[:, cols], in_=o_codes[:, cols].bitcast(I32))
        for q in range(4):
            queue = nc.scalar if q % 2 else nc.sync
            queue.dma_start(out=out_2[0, 4 * q : 4 * q + 4, :].bitcast(I32), in_=o_sc[32 * q : 32 * q + 4, :].bitcast(I32))
